import numpy as np
CORES = [73,201,329,457,330]
N = 5
TK = 128
D = 128 * N
EPS = 0.01
def setup_inputs(rng):
    return {"x": (rng.standard_normal((N, 128, TK), dtype=np.float32) * (0.5 + np.abs(rng.standard_normal((1, 1, TK), dtype=np.float32))) + rng.standard_normal((1, 1, TK), dtype=np.float32))}
def setup_inputs_big(rng):
    d = setup_inputs(rng)
    for k in ("x",): d[k] = (d[k].astype(np.float32) * 1024.0).astype(d[k].dtype)
    return d
def setup_inputs_small(rng):
    d = setup_inputs(rng)
    for k in ("x",): d[k] = (d[k].astype(np.float32) * (1 / 1024.0)).astype(d[k].dtype)
    return d
def setup_inputs_apart(rng):
    d = setup_inputs(rng)
    f = (10.0 ** rng.permutation(np.linspace(-1.5, 1.5, N))).astype(np.float32).reshape(N, 1, 1)
    for k in ("x",): d[k] = (d[k].astype(np.float32) * f).astype(d[k].dtype)
    return d
def setup_inputs_mixed(rng):
    d = setup_inputs(rng)
    f = (10.0 ** rng.uniform(-3, 3, (1, 1, TK))).astype(np.float32); shape = rng.integers(3, size=(1, 1, TK))
    for k in ("x",):
        x = d[k].astype(np.float32)
        m = x.mean(axis=(0, 1), keepdims=True); level = m + np.sign(x - m) * np.abs(x - m).mean(axis=(0, 1), keepdims=True) * rng.uniform(0.9, 1.1, x.shape).astype(np.float32)
        other = x * np.where(rng.random(x.shape) < 0.5, 0.1, 1.0).astype(np.float32)
        d[k] = (np.where(shape == 1, level, np.where(shape == 2, other, x)) * f).astype(d[k].dtype)
    return d
def setup_inputs_offset(rng):
    d = setup_inputs(rng)
    x = d["x"]; spread = x.std(axis=(0, 1), keepdims=True)
    d["x"] = (x + spread * rng.uniform(16, 48, (1, 1, TK)) * rng.choice([-1.0, 1.0], (1, 1, TK))).astype(np.float32)
    return d
def reference(x):
    X = x.astype(np.float64)
    mu = X.sum(axis=(0, 1)) / D
    Z = X - mu
    Z = Z / np.sqrt((Z ** 2).sum(axis=(0, 1)) / D + EPS)
    return {"y": Z.astype(np.float32)}

@@ -1,0 +1,206 @@
+import math
+from concourse.bass import DstId, RemoteDMATransfer
+from concourse.mybir import AluOpType, AxisListType, ActivationFunctionType
+
+F32 = "float32"
+SCRATCH = {
+    "xs": ("sbuf", [128, 128], F32),
+    "cst": ("sbuf", [128, 64], F32),
+    "dg": ("sbuf", [128, 64], F32),
+    "G": ("sbuf", [128, 24], F32),
+    "ja": ("sbuf", [128, 64], F32),
+    "jb": ("sbuf", [128, 64], F32),
+    "zl": ("sbuf", [128, 128], F32),
+    "zc": ("sbuf", [128, 128], F32),
+    "dgs": ("sbuf", [128, 64], F32),
+    "ys": ("sbuf", [128, 128], F32),
+    "dv": ("sbuf", [128, 12], F32),
+    "j10": ("sbuf", [128, 12], F32),
+    "sm": ("sbuf", [128, 16], F32),
+    "pa": ("psum", [128, 512], F32),
+    "pb": ("psum", [128, 512], F32),
+    "ya": ("psum", [128, 512], F32),
+    "yb": ("psum", [128, 512], F32),
+}
+_OPS = ["ld", "c0", "c1", "da", "db", "ta", "tb", "na", "nb", "qa", "qb", "e1", "e2", "e3", "e4", "e5", "e6", "e7", "e8",
+        "a1", "a2", "a3", "a4", "v1", "v2", "v3", "v4", "v5", "ma", "mb", "ca", "cb", "st"]
+SEMAPHORES = _OPS + ["rel", "arr", "snt"]
+
+EPS = 0.01
+
+
+def _bits(m):
+    return bin(m).count("1")
+
+
+def _plan(cores, topo):
+    n = len(cores)
+    order = sorted(range(n), key=lambda r: cores[r])
+    slot = {r: i for i, r in enumerate(order)}
+    ok = lambda a, b: topo.may_write(cores[a], cores[b])
+    jobs = {}
+    for s in range(n):
+        for d in range(n):
+            if s != d and not ok(s, d):
+                j = jobs.setdefault((topo.host(cores[s]), topo.host(cores[d])), (set(), set()))
+                j[0].add(s)
+                j[1].add(d)
+    load = [0] * n
+    job = {}
+    crit = {r: [] for r in range(n)}
+    for key in sorted(jobs):
+        srcs, dsts = jobs[key]
+        cands = [m for m in range(n) if m not in srcs and m not in dsts
+                 and all(ok(s, m) for s in srcs) and all(ok(m, d) for d in dsts)]
+        m = min(cands, key=lambda c: (load[c], c))
+        assert load[m] == 0
+        load[m] += 1
+        srcs = sorted(srcs, key=lambda r: slot[r])
+        assert slot[srcs[-1]] - slot[srcs[0]] == len(srcs) - 1
+        job[m] = (srcs, sorted(dsts))
+        for s in srcs:
+            crit[s].append(m)
+    direct = {s: [d for d in range(n) if d != s and ok(s, d) and d not in crit[s]] for s in range(n)}
+    return slot, crit, direct, job
+
+
+def rank_program(g, core, T, topo):
+    rank = T.rank_of(core)
+    if rank is None:
+        return
+    cores = list(T.cores)
+    n = len(cores)
+    nb = 2 * n
+    dtot = 64.0 * nb
+    slot, crit, direct, job = _plan(cores, topo)
+    A, X, ACT = AluOpType, AxisListType.X, ActivationFunctionType
+    V, S, P, Y = g.vector, g.scalar, g.tensor, g.sync
+    cnt = {}
+
+    def done(ins, name, k=1):
+        ins.then_inc(T.sem[name], k)
+        cnt[name] = cnt.get(name, 0) + k
+
+    def need(q, *names):
+        for nm in names:
+            q.wait_ge(T.sem[nm], cnt[nm])
+
+    def mask_to(dsts):
+        m = topo.mask(core, cores[dsts[0]])
+        for d in dsts[1:]:
+            m &= topo.mask(core, cores[d])
+        return m
+
+    def send(cols, dsts, sem):
+        m = mask_to(dsts)
+        ids = []
+        for d in dsts:
+            rid, pid = topo.addr(cores[d], core)
+            ids.append(DstId(rid=rid, pnc=pid))
+        ap = T.G[:, cols[0]:cols[1]]
+        g.remote_dma_fused([RemoteDMATransfer(dst_ids=ids, dma_engine_mask=m, remote_sem=T.sem[sem],
+                                              srcs=[ap], dsts=[ap for _ in dsts], alu_op=0)], local_sem=T.sem.snt)
+        cnt["snt"] = cnt.get("snt", 0) + _bits(m)
+
+    def eng(a, dsts):
+        m = topo.mask(cores[a], cores[dsts[0]])
+        for d in dsts[1:]:
+            m &= topo.mask(cores[a], cores[d])
+        return _bits(m)
+    rel_total = sum(eng(s, crit[s]) for s in range(n) if rank in crit[s])
+    arr_total = sum(eng(s, direct[s]) for s in range(n) if rank in direct[s])
+    arr_total += sum(eng(m, job[m][1]) for m in job if rank in job[m][1])
+
+    c0 = 4 * slot[rank]
+    nm_a, m2_a = T.G[:, c0:c0 + 1], T.G[:, c0 + 1:c0 + 2]
+    nm_b, m2_b = T.G[:, c0 + 2:c0 + 3], T.G[:, c0 + 3:c0 + 4]
+    col = lambda i: T.sm[:, i:i + 1]
+    mref, se, r, q, qn, kap, sd, sdd, smp, b, b2, t, rt = [col(i) for i in range(13)]
+    weps = dtot * EPS
+
+    done(Y.dma_start(T.xs[:], T.x[:]), "ld", 16)
+    done(V.memset(T.cst[:], 1.0 / 64.0), "c0")
+    done(V.memset(T.G[:, 4 * n:4 * n + 4], weps), "c1")
+    need(g, "c0")
+    done(g.affine_select(T.dg[0:64, :], T.cst[0:64, :], [[-1, 64]], A.is_equal, 0.0, 0, 1), "da")
+    done(g.affine_select(T.dg[64:128, :], T.cst[64:128, :], [[-1, 64]], A.is_equal, 0.0, 0, 1), "db")
+
+    need(P, "ld", "da")
+    done(P.matmul(T.pa[:, 0:64], T.xs[0:64, :], T.dg[0:64, :], True, True), "ta")
+    need(P, "db")
+    done(P.matmul(T.pb[:, 0:64], T.xs[64:128, :], T.dg[64:128, :], True, True), "tb")
+    need(V, "ta")
+    done(V.tensor_reduce(nm_a, T.pa[:, 0:64], X, A.add, negate=True), "na")
+    need(S, "na")
+    done(S.activation(T.ja[:], T.pa[:, 0:64], ACT.Square, bias=nm_a, scale=64.0, accum_out=m2_a), "qa")
+    need(V, "tb")
+    done(V.tensor_reduce(nm_b, T.pb[:, 0:64], X, A.add, negate=True), "nb")
+    need(S, "nb")
+    done(S.activation(T.jb[:], T.pb[:, 0:64], ACT.Square, bias=nm_b, scale=64.0, accum_out=m2_b), "qb")
+
+    need(g, "qa", "qb")
+    own = (c0, c0 + 4)
+    if crit[rank]:
+        send(own, crit[rank], "rel")
+    if direct[rank]:
+        send(own, direct[rank], "arr")
+
+    need(V, "na")
+    done(V.tensor_scalar(mref, nm_a, -1.0, None, A.mult), "e1")
+    need(S, "qa")
+    done(S.activation(se, m2_a, ACT.Sqrt, bias=weps, scale=1.0), "e4")
+    need(V, "qa")
+    done(V.tensor_scalar(T.zl[:, 0:64], T.pa[:, 0:64], 64.0, nm_a, A.mult, A.add), "e2")
+    need(V, "qb")
+    done(V.tensor_scalar(T.zl[:, 64:128], T.pb[:, 0:64], 64.0, nm_a, A.mult, A.add), "e3")
+    need(V, "e4")
+    done(V.reciprocal(r, se), "e5")
+    need(V, "e5")
+    done(V.tensor_tensor(q, r, r, A.mult), "e6")
+    done(V.tensor_scalar(qn, r, r, -64.0 / nb, A.mult, A.mult), "e7")
+    done(V.tensor_scalar(kap, r, 64.0 * math.sqrt(dtot) / nb, None, A.mult), "e8")
+
+    if rank in job:
+        srcs, dsts = job[rank]
+        g.wait_ge(T.sem.rel, rel_total)
+        send((4 * slot[srcs[0]], 4 * slot[srcs[-1]] + 4), dsts, "arr")
+
+    for qu in (S, V):
+        if rel_total:
+            qu.wait_ge(T.sem.rel, rel_total)
+        qu.wait_ge(T.sem.arr, arr_total)
+    need(S, "e1")
+    done(S.activation(T.dv[:, 0:nb], T.G[:, 0:2 * nb:2], ACT.Identity, bias=mref, scale=1.0, accum_out=sd), "a1")
+    need(V, "c1")
+    done(V.tensor_reduce(smp, T.G[:, 1:2 * nb + 2:2], X, A.add), "v1")
+    need(S, "a1")
+    done(S.activation(T.j10[:, 0:nb], T.dv[:, 0:nb], ACT.Square, scale=8.0, accum_out=sdd), "a2")
+    need(V, "a1", "e7")
+    done(V.tensor_scalar(b, sd, sd, qn, A.mult, A.mult), "v2")
+    need(V, "v1", "v2", "e6")
+    done(V.tensor_scalar(b2, smp, q, b, A.mult, A.add), "v3")
+    need(S, "a2", "v3", "e6")
+    done(S.activation(t, sdd, ACT.Sqrt, bias=b2, scale=q), "a3")
+    need(S, "e2", "e3")
+    done(S.activation(T.zc[:], T.zl[:], ACT.Identity, bias=sd, scale=float(nb)), "a4")
+    need(V, "a3")
+    done(V.reciprocal(rt, t), "v4")
+    need(V, "v4", "e8", "da", "db")
+    done(V.tensor_scalar(T.dgs[:], T.dg[:], rt, kap, A.mult, A.mult), "v5")
+
+    need(P, "a4", "v5")
+    done(P.matmul(T.ya[:, 0:64], T.zc[0:64, :], T.dgs[0:64, :], True, True), "ma")
+    done(P.matmul(T.yb[:, 0:64], T.zc[64:128, :], T.dgs[64:128, :], True, True), "mb")
+    need(V, "ma")
+    done(V.tensor_copy(T.ys[:, 0:64], T.ya[:, 0:64]), "ca")
+    need(V, "mb")
+    done(V.tensor_copy(T.ys[:, 64:128], T.yb[:, 0:64]), "cb")
+    need(Y, "ca", "cb")
+    done(Y.dma_start(T.y[:], T.ys[:]), "st", 16)
+    need(Y, "st")
+
+    need(g, "snt")
+    if rel_total:
+        g.wait_ge(T.sem.rel, rel_total)
+    g.wait_ge(T.sem.arr, arr_total)
+    need(g, "st")

@@ -4,7 +4,7 @@ from concourse.mybir import AluOpType, AxisListType, ActivationFunctionType
 
 F32 = "float32"
 SCRATCH = {
-    "xs": ("sbuf", [128, 128], F32),
+    "xs": ("sbuf", [128, 256], F32),
     "cst": ("sbuf", [128, 64], F32),
     "dg": ("sbuf", [128, 64], F32),
     "G": ("sbuf", [128, 24], F32),
@@ -22,8 +22,8 @@ SCRATCH = {
     "ya": ("psum", [128, 512], F32),
     "yb": ("psum", [128, 512], F32),
 }
-_OPS = ["ld", "c0", "c1", "da", "db", "ta", "tb", "na", "nb", "qa", "qb", "e1", "e2", "e3", "e4", "e5", "e6", "e7", "e8",
-        "a1", "a2", "a3", "a4", "v1", "v2", "v3", "v4", "v5", "ma", "mb", "ca", "cb", "st"]
+_OPS = ["lda", "ldb", "c0", "c1", "da", "db", "ta", "tb", "na", "nb", "qa", "qb", "e1", "e2", "e3", "e4", "e5", "e6", "e7",
+        "e8", "a1", "a2", "a3", "a4", "v1", "v3", "v4", "v5", "ma", "mb", "ca", "cb", "sta", "stb"]
 SEMAPHORES = _OPS + ["rel", "arr", "snt"]
 
 EPS = 0.01
@@ -115,20 +115,21 @@ def rank_program(g, core, T, topo):
     nm_a, m2_a = T.G[:, c0:c0 + 1], T.G[:, c0 + 1:c0 + 2]
     nm_b, m2_b = T.G[:, c0 + 2:c0 + 3], T.G[:, c0 + 3:c0 + 4]
     col = lambda i: T.sm[:, i:i + 1]
-    mref, se, r, q, qn, kap, sd, sdd, smp, b, b2, t, rt = [col(i) for i in range(13)]
+    mref, se, r, q, qs, kap, sd, sdd, smp, smq, t, rt = [col(i) for i in range(12)]
     weps = dtot * EPS
 
-    done(Y.dma_start(T.xs[:], T.x[:]), "ld", 16)
+    done(Y.dma_start(T.xs[0:64, 0:128], T.x[0:64, :]), "lda", 16)
+    done(S.dma_start(T.xs[0:64, 128:256], T.x[64:128, :]), "ldb", 16)
     done(V.memset(T.cst[:], 1.0 / 64.0), "c0")
     done(V.memset(T.G[:, 4 * n:4 * n + 4], weps), "c1")
     need(g, "c0")
     done(g.affine_select(T.dg[0:64, :], T.cst[0:64, :], [[-1, 64]], A.is_equal, 0.0, 0, 1), "da")
     done(g.affine_select(T.dg[64:128, :], T.cst[64:128, :], [[-1, 64]], A.is_equal, 0.0, 0, 1), "db")
 
-    need(P, "ld", "da")
-    done(P.matmul(T.pa[:, 0:64], T.xs[0:64, :], T.dg[0:64, :], True, True), "ta")
-    need(P, "db")
-    done(P.matmul(T.pb[:, 0:64], T.xs[64:128, :], T.dg[64:128, :], True, True), "tb")
+    need(P, "lda", "da")
+    done(P.matmul(T.pa[:, 0:64], T.xs[0:64, 0:128], T.dg[0:64, :], True, True), "ta")
+    need(P, "ldb")
+    done(P.matmul(T.pb[:, 0:64], T.xs[0:64, 128:256], T.dg[0:64, :], True, True), "tb")
     need(V, "ta")
     done(V.tensor_reduce(nm_a, T.pa[:, 0:64], X, A.add, negate=True), "na")
     need(S, "na")
@@ -157,7 +158,7 @@ def rank_program(g, core, T, topo):
     done(V.reciprocal(r, se), "e5")
     need(V, "e5")
     done(V.tensor_tensor(q, r, r, A.mult), "e6")
-    done(V.tensor_scalar(qn, r, r, -64.0 / nb, A.mult, A.mult), "e7")
+    done(V.tensor_scalar(qs, r, r, 64.0 / (nb * nb), A.mult, A.mult), "e7")
     done(V.tensor_scalar(kap, r, 64.0 * math.sqrt(dtot) / nb, None, A.mult), "e8")
 
     if rank in job:
@@ -174,13 +175,11 @@ def rank_program(g, core, T, topo):
     need(V, "c1")
     done(V.tensor_reduce(smp, T.G[:, 1:2 * nb + 2:2], X, A.add), "v1")
     need(S, "a1")
-    done(S.activation(T.j10[:, 0:nb], T.dv[:, 0:nb], ACT.Square, scale=8.0, accum_out=sdd), "a2")
-    need(V, "a1", "e7")
-    done(V.tensor_scalar(b, sd, sd, qn, A.mult, A.mult), "v2")
-    need(V, "v1", "v2", "e6")
-    done(V.tensor_scalar(b2, smp, q, b, A.mult, A.add), "v3")
-    need(S, "a2", "v3", "e6")
-    done(S.activation(t, sdd, ACT.Sqrt, bias=b2, scale=q), "a3")
+    done(S.activation(T.j10[:, 0:nb], T.dv[:, 0:nb], ACT.Square, bias=sd, scale=-float(nb), accum_out=sdd), "a2")
+    need(V, "v1", "e6")
+    done(V.tensor_scalar(smq, smp, q, None, A.mult), "v3")
+    need(S, "a2", "v3", "e7")
+    done(S.activation(t, sdd, ACT.Sqrt, bias=smq, scale=qs), "a3")
     need(S, "e2", "e3")
     done(S.activation(T.zc[:], T.zl[:], ACT.Identity, bias=sd, scale=float(nb)), "a4")
     need(V, "a3")
@@ -193,14 +192,17 @@ def rank_program(g, core, T, topo):
     done(P.matmul(T.yb[:, 0:64], T.zc[64:128, :], T.dgs[64:128, :], True, True), "mb")
     need(V, "ma")
     done(V.tensor_copy(T.ys[:, 0:64], T.ya[:, 0:64]), "ca")
+    need(Y, "ca")
+    done(Y.dma_start(T.y[:, 0:64], T.ys[:, 0:64]), "sta", 16)
     need(V, "mb")
     done(V.tensor_copy(T.ys[:, 64:128], T.yb[:, 0:64]), "cb")
-    need(Y, "ca", "cb")
-    done(Y.dma_start(T.y[:], T.ys[:]), "st", 16)
-    need(Y, "st")
+    need(S, "cb")
+    done(S.dma_start(T.y[:, 64:128], T.ys[:, 64:128]), "stb", 16)
+    need(Y, "sta")
+    need(S, "stb")
 
     need(g, "snt")
     if rel_total:
         g.wait_ge(T.sem.rel, rel_total)
     g.wait_ge(T.sem.arr, arr_total)
-    need(g, "st")
+    need(g, "sta", "stb")

import math
from concourse.bass import DstId, RemoteDMATransfer
from concourse.mybir import AluOpType, AxisListType, ActivationFunctionType

F32 = "float32"
SCRATCH = {
    "xs": ("sbuf", [128, 256], F32),
    "cst": ("sbuf", [128, 64], F32),
    "dg": ("sbuf", [128, 64], F32),
    "G": ("sbuf", [128, 24], F32),
    "ja": ("sbuf", [128, 64], F32),
    "jb": ("sbuf", [128, 64], F32),
    "zl": ("sbuf", [128, 128], F32),
    "zc": ("sbuf", [128, 128], F32),
    "dgs": ("sbuf", [128, 64], F32),
    "ys": ("sbuf", [128, 128], F32),
    "dv": ("sbuf", [128, 12], F32),
    "j10": ("sbuf", [128, 12], F32),
    "sm": ("sbuf", [128, 16], F32),
    "pa": ("psum", [128, 512], F32),
    "pb": ("psum", [128, 512], F32),
    "ya": ("psum", [128, 512], F32),
    "yb": ("psum", [128, 512], F32),
}
_OPS = ["lda", "ldb", "c0", "c1", "da", "db", "ta", "tb", "na", "nb", "qa", "qb", "e1", "e2", "e3", "e4", "e5", "e6", "e7",
        "e8", "a1", "a2", "a3", "a4", "v1", "v3", "v4", "v5", "ma", "mb", "ca", "cb", "sta", "stb"]
SEMAPHORES = _OPS + ["rel", "arr", "snt"]

EPS = 0.01


def _bits(m):
    return bin(m).count("1")


def _plan(cores, topo):
    n = len(cores)
    order = sorted(range(n), key=lambda r: cores[r])
    slot = {r: i for i, r in enumerate(order)}
    ok = lambda a, b: topo.may_write(cores[a], cores[b])
    jobs = {}
    for s in range(n):
        for d in range(n):
            if s != d and not ok(s, d):
                j = jobs.setdefault((topo.host(cores[s]), topo.host(cores[d])), (set(), set()))
                j[0].add(s)
                j[1].add(d)
    load = [0] * n
    job = {}
    crit = {r: [] for r in range(n)}
    for key in sorted(jobs):
        srcs, dsts = jobs[key]
        cands = [m for m in range(n) if m not in srcs and m not in dsts
                 and all(ok(s, m) for s in srcs) and all(ok(m, d) for d in dsts)]
        m = min(cands, key=lambda c: (load[c], c))
        assert load[m] == 0
        load[m] += 1
        srcs = sorted(srcs, key=lambda r: slot[r])
        assert slot[srcs[-1]] - slot[srcs[0]] == len(srcs) - 1
        job[m] = (srcs, sorted(dsts))
        for s in srcs:
            crit[s].append(m)
    direct = {s: [d for d in range(n) if d != s and ok(s, d) and d not in crit[s]] for s in range(n)}
    return slot, crit, direct, job


def rank_program(g, core, T, topo):
    rank = T.rank_of(core)
    if rank is None:
        return
    cores = list(T.cores)
    n = len(cores)
    nb = 2 * n
    dtot = 64.0 * nb
    slot, crit, direct, job = _plan(cores, topo)
    A, X, ACT = AluOpType, AxisListType.X, ActivationFunctionType
    V, S, P, Y = g.vector, g.scalar, g.tensor, g.sync
    cnt = {}

    def done(ins, name, k=1):
        ins.then_inc(T.sem[name], k)
        cnt[name] = cnt.get(name, 0) + k

    def need(q, *names):
        for nm in names:
            q.wait_ge(T.sem[nm], cnt[nm])

    def mask_to(dsts):
        m = topo.mask(core, cores[dsts[0]])
        for d in dsts[1:]:
            m &= topo.mask(core, cores[d])
        return m

    def send(cols, dsts, sem):
        m = mask_to(dsts)
        ids = []
        for d in dsts:
            rid, pid = topo.addr(cores[d], core)
            ids.append(DstId(rid=rid, pnc=pid))
        ap = T.G[:, cols[0]:cols[1]]
        g.remote_dma_fused([RemoteDMATransfer(dst_ids=ids, dma_engine_mask=m, remote_sem=T.sem[sem],
                                              srcs=[ap], dsts=[ap for _ in dsts], alu_op=0)], local_sem=T.sem.snt)
        cnt["snt"] = cnt.get("snt", 0) + _bits(m)

    def eng(a, dsts):
        m = topo.mask(cores[a], cores[dsts[0]])
        for d in dsts[1:]:
            m &= topo.mask(cores[a], cores[d])
        return _bits(m)
    rel_total = sum(eng(s, crit[s]) for s in range(n) if rank in crit[s])
    arr_total = sum(eng(s, direct[s]) for s in range(n) if rank in direct[s])
    arr_total += sum(eng(m, job[m][1]) for m in job if rank in job[m][1])

    c0 = 4 * slot[rank]
    nm_a, m2_a = T.G[:, c0:c0 + 1], T.G[:, c0 + 1:c0 + 2]
    nm_b, m2_b = T.G[:, c0 + 2:c0 + 3], T.G[:, c0 + 3:c0 + 4]
    col = lambda i: T.sm[:, i:i + 1]
    mref, se, r, q, qs, kap, sd, sdd, smp, smq, t, rt = [col(i) for i in range(12)]
    weps = dtot * EPS

    done(Y.dma_start(T.xs[0:64, 0:128], T.x[0:64, :]), "lda", 16)
    done(S.dma_start(T.xs[0:64, 128:256], T.x[64:128, :]), "ldb", 16)
    done(V.memset(T.cst[:], 1.0 / 64.0), "c0")
    done(V.memset(T.G[:, 4 * n:4 * n + 4], weps), "c1")
    need(g, "c0")
    done(g.affine_select(T.dg[0:64, :], T.cst[0:64, :], [[-1, 64]], A.is_equal, 0.0, 0, 1), "da")
    done(g.affine_select(T.dg[64:128, :], T.cst[64:128, :], [[-1, 64]], A.is_equal, 0.0, 0, 1), "db")

    need(P, "lda", "da")
    done(P.matmul(T.pa[:, 0:64], T.xs[0:64, 0:128], T.dg[0:64, :], True, True), "ta")
    need(P, "ldb")
    done(P.matmul(T.pb[:, 0:64], T.xs[0:64, 128:256], T.dg[0:64, :], True, True), "tb")
    need(V, "ta")
    done(V.tensor_reduce(nm_a, T.pa[:, 0:64], X, A.add, negate=True), "na")
    need(S, "na")
    done(S.activation(T.ja[:], T.pa[:, 0:64], ACT.Square, bias=nm_a, scale=64.0, accum_out=m2_a), "qa")
    need(V, "tb")
    done(V.tensor_reduce(nm_b, T.pb[:, 0:64], X, A.add, negate=True), "nb")
    need(S, "nb")
    done(S.activation(T.jb[:], T.pb[:, 0:64], ACT.Square, bias=nm_b, scale=64.0, accum_out=m2_b), "qb")

    need(g, "qa", "qb")
    own = (c0, c0 + 4)
    if crit[rank]:
        send(own, crit[rank], "rel")
    if direct[rank]:
        send(own, direct[rank], "arr")

    need(V, "na")
    done(V.tensor_scalar(mref, nm_a, -1.0, None, A.mult), "e1")
    need(S, "qa")
    done(S.activation(se, m2_a, ACT.Sqrt, bias=weps, scale=1.0), "e4")
    need(V, "qa")
    done(V.tensor_scalar(T.zl[:, 0:64], T.pa[:, 0:64], 64.0, nm_a, A.mult, A.add), "e2")
    need(V, "qb")
    done(V.tensor_scalar(T.zl[:, 64:128], T.pb[:, 0:64], 64.0, nm_a, A.mult, A.add), "e3")
    need(V, "e4")
    done(V.reciprocal(r, se), "e5")
    need(V, "e5")
    done(V.tensor_tensor(q, r, r, A.mult), "e6")
    done(V.tensor_scalar(qs, r, r, 64.0 / (nb * nb), A.mult, A.mult), "e7")
    done(V.tensor_scalar(kap, r, 64.0 * math.sqrt(dtot) / nb, None, A.mult), "e8")

    if rank in job:
        srcs, dsts = job[rank]
        g.wait_ge(T.sem.rel, rel_total)
        send((4 * slot[srcs[0]], 4 * slot[srcs[-1]] + 4), dsts, "arr")

    for qu in (S, V):
        if rel_total:
            qu.wait_ge(T.sem.rel, rel_total)
        qu.wait_ge(T.sem.arr, arr_total)
    need(S, "e1")
    done(S.activation(T.dv[:, 0:nb], T.G[:, 0:2 * nb:2], ACT.Identity, bias=mref, scale=1.0, accum_out=sd), "a1")
    need(V, "c1")
    done(V.tensor_reduce(smp, T.G[:, 1:2 * nb + 2:2], X, A.add), "v1")
    need(S, "a1")
    done(S.activation(T.j10[:, 0:nb], T.dv[:, 0:nb], ACT.Square, bias=sd, scale=-float(nb), accum_out=sdd), "a2")
    need(V, "v1", "e6")
    done(V.tensor_scalar(smq, smp, q, None, A.mult), "v3")
    need(S, "a2", "v3", "e7")
    done(S.activation(t, sdd, ACT.Sqrt, bias=smq, scale=qs), "a3")
    need(S, "e2", "e3")
    done(S.activation(T.zc[:], T.zl[:], ACT.Identity, bias=sd, scale=float(nb)), "a4")
    need(V, "a3")
    done(V.reciprocal(rt, t), "v4")
    need(V, "v4", "e8", "da", "db")
    done(V.tensor_scalar(T.dgs[:], T.dg[:], rt, kap, A.mult, A.mult), "v5")

    need(P, "a4", "v5")
    done(P.matmul(T.ya[:, 0:64], T.zc[0:64, :], T.dgs[0:64, :], True, True), "ma")
    done(P.matmul(T.yb[:, 0:64], T.zc[64:128, :], T.dgs[64:128, :], True, True), "mb")
    need(V, "ma")
    done(V.tensor_copy(T.ys[:, 0:64], T.ya[:, 0:64]), "ca")
    need(Y, "ca")
    done(Y.dma_start(T.y[:, 0:64], T.ys[:, 0:64]), "sta", 16)
    need(V, "mb")
    done(V.tensor_copy(T.ys[:, 64:128], T.yb[:, 0:64]), "cb")
    need(S, "cb")
    done(S.dma_start(T.y[:, 64:128], T.ys[:, 64:128]), "stb", 16)
    need(Y, "sta")
    need(S, "stb")

    need(g, "snt")
    if rel_total:
        g.wait_ge(T.sem.rel, rel_total)
    g.wait_ge(T.sem.arr, arr_total)
    need(g, "sta", "stb")
